import numpy as np
import ml_dtypes


def mxq(x, axis, fmt="e4m3"):
    dtype, down = {"e4m3": (ml_dtypes.float8_e4m3fn, 7), "e5m2": (ml_dtypes.float8_e5m2, 14)}[fmt]
    v = np.moveaxis(np.asarray(x, np.float32).astype(ml_dtypes.bfloat16).astype(np.float64), axis, -1)
    blocks = v.reshape(v.shape[:-1] + (-1, 32))
    amax = np.abs(blocks).max(-1, keepdims=True)
    byte = np.maximum(np.where(amax > 0, np.frexp(amax)[1] - 1 + 127, 0) - down, 1)
    scale = np.exp2(byte - 127.0)
    codes = (blocks / scale).astype(np.float32).astype(dtype).astype(np.float64)
    return np.moveaxis((codes * scale).reshape(v.shape), -1, axis)


WIDE = False


def mx_kscale(k):
    if not WIDE:
        return np.ones(k)
    levels = np.array([10, -10, 5, -5, 0])
    if k % 512:
        return np.exp2(np.random.permutation(np.resize(levels, k // 32))).repeat(32)
    a = np.empty((k // 512, 16))
    for p in range(k // 512):
        a[p, :8] = np.random.permutation(np.resize(levels, 8))
        for g in range(8):
            far = levels[np.abs(levels - a[p, g]) >= 10]
            a[p, g + 8] = far[np.random.randint(len(far))]
    return np.exp2(a.ravel()).repeat(32)


def f64(x):
    return np.asarray(x).astype(np.float64)


def striped(idx):
    return np.tile(np.asarray(idx).reshape(-1, 16).T, (8, 1)).astype(np.uint16)


def unstriped(offs):
    return offs[:16].T.reshape(-1).astype(np.int64)


E2M1 = np.array([0.0, 0.5, 1.0, 1.5, 2.0, 3.0, 4.0, 6.0, -0.0, -0.5, -1.0, -1.5, -2.0, -3.0, -4.0, -6.0])


def pack_weight(w, fmt):
    k, n = w.shape
    w = f64(np.asarray(w, np.float32).astype(ml_dtypes.bfloat16)).reshape(k // 32, 32, n)
    amax = np.abs(w).max(1)
    if fmt == "e4m3":
        byte = np.frexp(amax)[1] - 1 + 127 - 7
    else:
        mant, ex = np.frexp(amax / 6.0)
        byte = np.where(mant > 0.5, ex, ex - 1) + 127
    byte = np.clip(np.where(amax > 0, byte, 1), 1, 254)
    scaled = (w * np.exp2(127.0 - byte)[:, None, :]).reshape(k, n).astype(np.float32)
    by_word = np.ascontiguousarray(scaled.reshape(k // 512, 128, 4, n).transpose(0, 1, 3, 2))
    if fmt == "e4m3":
        words = by_word.astype(ml_dtypes.float8_e4m3fn).view(np.uint8)
    else:
        c = by_word.astype(ml_dtypes.float4_e2m1fn).view(np.uint8) & 0xF
        words = (c[..., 0::2] | (c[..., 1::2] << 4)).reshape(k // 512, 128, 2 * n)
    return np.ascontiguousarray(words), np.ascontiguousarray(byte.astype(np.uint8).reshape(k // 512, 16, n))


def unpack_weight(words, scales, fmt):
    g, _, n = scales.shape
    words = np.ascontiguousarray(words).reshape(g, 128, n, -1)
    if fmt == "e4m3":
        vals = words.view(ml_dtypes.float8_e4m3fn).astype(np.float64)
    else:
        nib = np.empty((g, 128, n, 4), np.uint8)
        nib[..., 0::2] = words & 0xF
        nib[..., 1::2] = words >> 4
        vals = E2M1[nib]
    vals = vals * np.repeat(np.exp2(scales.astype(np.float64) - 127.0), 8, axis=1)[..., None]
    return vals.transpose(0, 1, 3, 2).reshape(g * 512, n)


D, E, T, I, Q = 512, 512, 2048, 512, 128


def setup_inputs():
    n = np.random.standard_normal
    idx = np.random.permutation(T)[:I]
    fd = mx_kscale(D)
    fe = mx_kscale(E)
    keysp = pack_weight(n((D, T)) / fd[:, None], "e2m1")
    valsp = pack_weight(n((E, T)) / fe[:, None], "e2m1")
    return {
        "query": (n((D, Q)) * 0.7 / np.sqrt(D) * fd[:, None]).astype(np.float32),
        "keys_words": keysp[0],
        "keys_scales": keysp[1],
        "gout": (n((E, Q)) * 1 / np.sqrt(E) * fe[:, None]).astype(np.float32),
        "vals_words": valsp[0],
        "vals_scales": valsp[1],
        "old": (0.5 * n((Q, T))).astype(np.float32),
        "offs": striped(idx),
    }


def reference(query, keys_words, keys_scales, gout, vals_words, vals_scales, old, offs):
    idx = unstriped(offs)
    keysu = unpack_weight(keys_words, keys_scales, "e2m1")
    valsu = unpack_weight(vals_words, vals_scales, "e2m1")
    queryq = mxq(f64(query), 0, "e4m3")
    keysidxg = keysu[:, idx]
    a = queryq.T @ keysidxg
    p = np.exp(a - np.max(a, axis=1, keepdims=True))
    n2 = np.sqrt(np.sum(np.square(p), axis=1, keepdims=True))
    goutq = mxq(f64(gout), 0, "e4m3")
    valsidxg = valsu[:, idx]
    c0 = goutq.T @ valsidxg
    dn2 = np.sum(c0 * p / np.square(n2) * (-1.0), axis=1, keepdims=True)
    dp = c0 / n2 + dn2 * 0.5 / np.sqrt(np.sum(np.square(p), axis=1, keepdims=True)) * p * 2.0
    da = dp * p
    gs = da * 16.0
    gf = np.zeros((Q, T))
    gf[:, idx] = gs
    y = f64(old) + gf
    return y

import math
from contextlib import ExitStack

import concourse.mybir as mybir

D, E, T, I, Q = 512, 512, 2048, 512, 128
FLOPS = 2 * Q * I * (D + E)

F32 = mybir.dt.float32
BF16 = mybir.dt.bfloat16
I32 = mybir.dt.int32
U32 = mybir.dt.uint32
U16 = mybir.dt.uint16
U8 = mybir.dt.uint8
FP8X4 = mybir.dt.float8_e4m3fn_x4
FP4X4 = mybir.dt.float4_e2m1fn_x4
ALU = mybir.AluOpType
ACT = mybir.ActivationFunctionType
AX = mybir.AxisListType

P = 128
PACK = 4
CHUNKS = (256, 512, 512, 512, 256)


def tile_attend_bunitweights_s_kernel(tc, query, keys_words, keys_scales, gout, vals_words, vals_scales, old, offs, out):
    nc = tc.nc
    with ExitStack() as ctx:
        sb = ctx.enter_context(tc.tile_pool(name="sb", bufs=1))
        ps = ctx.enter_context(tc.psum_pool(name="ps", bufs=1))

        offsets = sb.tile([P, I // 16], U16, name="offsets")
        nc.sync.dma_start(offsets[:], offs)

        def load_words(name, words):
            t = sb.tile([P, T], U16, name=name, align_bytes=64)
            nc.sync.dma_start(out=t[:].bitcast(I32), in_=words[0].bitcast(I32))
            return t

        def load_scales(name, scales):
            t = sb.tile([P, T], U8, name=name, align_bytes=64)
            nc.vector.memset(t[:].bitcast(I32), 0)
            for quad in range(4):
                nc.sync.dma_start(out=t[32 * quad : 32 * quad + 4, :].bitcast(I32), in_=scales[0, 4 * quad : 4 * quad + 4, :].bitcast(I32))
            return t

        def load_rows(name, rows):
            t = sb.tile([P, PACK, Q], F32, name=name)
            nc.sync.dma_start(out=t[:], in_=rows.rearrange("(p j) w -> p j w", j=PACK))
            return t

        def weave(name, raw):
            t = sb.tile([P, Q, PACK], BF16, name=name, align_bytes=64)
            nc.scalar.activation(out=t[:].rearrange("p (c i) j -> p c j i", i=4), in_=raw[:].rearrange("p j (c i) -> p c j i", i=4), func=ACT.Copy)
            return t

        def quantize(name, woven, tag):
            codes = sb.tile([P, Q], U32, name=name + "_codes", tag=tag, align_bytes=64)
            scales = sb.tile([P, Q], U8, name=name + "_scales", align_bytes=64)
            nc.vector.quantize_mx(out=codes[:].bitcast(FP8X4), scales=scales[:], in_=woven[:].rearrange("p w j -> p (w j)"))
            return codes, scales

        def gather(name, pool_tile, dtype):
            t = sb.tile([P, I], dtype, name=name, align_bytes=64)
            nc.vector.tensor_copy(t[:], pool_tile[:].indirect(offsets[:]))
            return t

        def product(name, codes, scales, words, word_scales):
            acc = ps.tile([Q, I], F32, name=name)
            nc.tensor.matmul_mx(out=acc[:], lhsT=codes[:].bitcast(FP8X4), lhsT_scale=scales[:],
                                rhs=words[:].bitcast(FP4X4), rhs_scale=word_scales[:], start=True, stop=True)
            return acc

        kw = load_words("kw", keys_words)
        ks = load_scales("ks", keys_scales)
        q_raw = load_rows("q_raw", query)
        g_raw = load_rows("g_raw", gout)
        vs = load_scales("vs", vals_scales)
        vw = load_words("vw", vals_words)
        old_sb = sb.tile([Q, T], F32, name="old_sb")
        nc.sync.dma_start(out=old_sb[:], in_=old)

        gf = sb.tile([Q, T], F32, name="gf")
        nc.vector.memset(gf[:], 0.0)
        half = sb.tile([Q, 1], F32, name="half")
        nc.gpsimd.memset(half[:], -0.5)

        kwg = gather("kwg", kw, U16)
        ksg = gather("ksg", ks, U8)
        qc, qs = quantize("q", weave("q_woven", q_raw), "shared")
        a = product("a", qc, qs, kwg, ksg)
        g_woven = weave("g_woven", g_raw)
        vsg = gather("vsg", vs, U8)
        gc, gsc = quantize("g", g_woven, "g_codes")

        x = sb.tile([Q, I], F32, name="x")
        b2 = sb.tile([Q, 1], F32, name="b2")
        nc.vector.tensor_scalar(out=x[:], in0=a[:], scalar1=-2.0, scalar2=None, op0=ALU.mult, op1=ALU.min, accum_out=b2[:])
        p2 = sb.tile([Q, I], F32, name="p2")
        ssum = sb.tile([Q, 1], F32, name="ssum")
        nc.scalar.activation(out=p2[:], in_=x[:], func=ACT.Exp, bias=b2[:], scale=-1.0, accum_out=ssum[:])
        b1 = sb.tile([Q, 1], F32, name="b1")
        nc.scalar.activation(out=b1[:], in_=b2[:], func=ACT.Copy, bias=math.log(16.0), scale=0.5)
        p = sb.tile([Q, I], F32, name="p")
        nc.scalar.activation(out=p[:], in_=x[:], func=ACT.Exp, bias=b1[:], scale=-0.5)
        s = sb.tile([Q, 1], F32, name="s")
        nc.gpsimd.tensor_tensor(out=s[:], in0=ssum[:], in1=half[:], op=ALU.pow)
        k = sb.tile([Q, 1], F32, name="k")
        nc.gpsimd.tensor_scalar(out=k[:], in0=s[:], scalar1=s[:], scalar2=-1.0, op0=ALU.mult, op1=ALU.mult)

        vwg = sb.tile([P, I], U16, name="vwg", tag="shared", align_bytes=64)
        c0 = ps.tile([Q, I], F32, name="c0")
        H = I // 2
        for h in range(2):
            cols = slice(h * H, (h + 1) * H)
            nc.vector.tensor_copy(vwg[:, cols], vw[:].indirect(offsets[:, h * H // 16 : (h + 1) * H // 16]))
            nc.tensor.matmul_mx(out=c0[:, cols], lhsT=gc[:].bitcast(FP8X4), lhsT_scale=gsc[:],
                                rhs=vwg[:, cols].bitcast(FP4X4), rhs_scale=vsg[:, cols], start=True, stop=True)

        u = sb.tile([Q, I], F32, name="u")
        dsum = sb.tile([Q, 1], F32, name="dsum")
        nc.vector.scalar_tensor_tensor(out=u[:], in0=c0[:], scalar=s[:], in1=p[:], op0=ALU.mult, op1=ALU.mult, accum_out=dsum[:])
        v = sb.tile([Q, I], F32, name="v")
        nc.vector.tensor_scalar(out=v[:], in0=p2[:], scalar1=dsum[:], scalar2=k[:], op0=ALU.mult, op1=ALU.mult)
        nc.vector.tensor_tensor(gf[:].indirect(offsets[:]), u[:], v[:], ALU.add)

        c = 0
        for j, w in enumerate(CHUNKS):
            r = sb.tile([Q, w], F32, name="res%d" % j)
            nc.vector.tensor_tensor(out=r[:], in0=gf[:, c : c + w], in1=old_sb[:, c : c + w], op=ALU.add)
            nc.sync.dma_start(out=out[:, c : c + w], in_=r[:])
            c = c + w
